import numpy as np
import ml_dtypes


def mxq(x, axis, fmt="e4m3"):
    dtype, down = {"e4m3": (ml_dtypes.float8_e4m3fn, 7), "e5m2": (ml_dtypes.float8_e5m2, 14)}[fmt]
    v = np.moveaxis(np.asarray(x, np.float32).astype(ml_dtypes.bfloat16).astype(np.float64), axis, -1)
    blocks = v.reshape(v.shape[:-1] + (-1, 32))
    amax = np.abs(blocks).max(-1, keepdims=True)
    byte = np.maximum(np.where(amax > 0, np.frexp(amax)[1] - 1 + 127, 0) - down, 1)
    scale = np.exp2(byte - 127.0)
    codes = (blocks / scale).astype(np.float32).astype(dtype).astype(np.float64)
    return np.moveaxis((codes * scale).reshape(v.shape), -1, axis)


WIDE = False


def mx_kscale(k):
    if not WIDE:
        return np.ones(k)
    levels = np.array([10, -10, 5, -5, 0])
    if k % 512:
        return np.exp2(np.random.permutation(np.resize(levels, k // 32))).repeat(32)
    a = np.empty((k // 512, 16))
    for p in range(k // 512):
        a[p, :8] = np.random.permutation(np.resize(levels, 8))
        for g in range(8):
            far = levels[np.abs(levels - a[p, g]) >= 10]
            a[p, g + 8] = far[np.random.randint(len(far))]
    return np.exp2(a.ravel()).repeat(32)


def f64(x):
    return np.asarray(x).astype(np.float64)


def striped8(idx):
    return np.asarray(idx).reshape(8, -1, 16).transpose(0, 2, 1).reshape(128, -1).astype(np.uint16)


def unstriped8(offs):
    return offs.reshape(8, 16, -1).transpose(0, 2, 1).reshape(8, -1).astype(np.int64)


def pick8(x, idx, run):
    r = np.arange(len(x))
    return x[r[:, None], idx[r % (8 * run) // run]]


E2M1 = np.array([0.0, 0.5, 1.0, 1.5, 2.0, 3.0, 4.0, 6.0, -0.0, -0.5, -1.0, -1.5, -2.0, -3.0, -4.0, -6.0])


def pack_weight(w, fmt):
    k, n = w.shape
    w = f64(np.asarray(w, np.float32).astype(ml_dtypes.bfloat16)).reshape(k // 32, 32, n)
    amax = np.abs(w).max(1)
    if fmt == "e4m3":
        byte = np.frexp(amax)[1] - 1 + 127 - 7
    else:
        mant, ex = np.frexp(amax / 6.0)
        byte = np.where(mant > 0.5, ex, ex - 1) + 127
    byte = np.clip(np.where(amax > 0, byte, 1), 1, 254)
    scaled = (w * np.exp2(127.0 - byte)[:, None, :]).reshape(k, n).astype(np.float32)
    by_word = np.ascontiguousarray(scaled.reshape(k // 512, 128, 4, n).transpose(0, 1, 3, 2))
    if fmt == "e4m3":
        words = by_word.astype(ml_dtypes.float8_e4m3fn).view(np.uint8)
    else:
        c = by_word.astype(ml_dtypes.float4_e2m1fn).view(np.uint8) & 0xF
        words = (c[..., 0::2] | (c[..., 1::2] << 4)).reshape(k // 512, 128, 2 * n)
    return np.ascontiguousarray(words), np.ascontiguousarray(byte.astype(np.uint8).reshape(k // 512, 16, n))


def unpack_weight(words, scales, fmt):
    g, _, n = scales.shape
    words = np.ascontiguousarray(words).reshape(g, 128, n, -1)
    if fmt == "e4m3":
        vals = words.view(ml_dtypes.float8_e4m3fn).astype(np.float64)
    else:
        nib = np.empty((g, 128, n, 4), np.uint8)
        nib[..., 0::2] = words & 0xF
        nib[..., 1::2] = words >> 4
        vals = E2M1[nib]
    vals = vals * np.repeat(np.exp2(scales.astype(np.float64) - 127.0), 8, axis=1)[..., None]
    return vals.transpose(0, 1, 3, 2).reshape(g * 512, n)


D, T, I, Q = 512, 1024, 512, 128


def setup_inputs():
    n = np.random.standard_normal
    idx = np.stack([np.random.permutation(T)[:I] for _ in range(8)])
    idx2 = np.stack([np.random.permutation(T)[:I] for _ in range(8)])
    idx3 = np.stack([np.random.permutation(T)[:I] for _ in range(8)])
    fd = mx_kscale(D)
    keysp = pack_weight(n((D, T)) / fd[:, None], "e2m1")
    return {
        "query": (n((D, Q)) * 1.0 / np.sqrt(D) * fd[:, None]).astype(np.float32),
        "keys_words": keysp[0],
        "keys_scales": keysp[1],
        "lam": (np.random.uniform(0.4, 1.0, (Q, 1))).astype(np.float32),
        "pull": (np.random.uniform(0.3, 0.9, (Q, 1))).astype(np.float32),
        "old": (np.random.uniform(0.0, 2.0, (Q, T))).astype(np.float32),
        "fade": (np.random.uniform(0.3, 0.9, (Q, 1))).astype(np.float32),
        "offs": striped8(idx),
        "offs2": striped8(idx2),
        "offs3": striped8(idx3),
    }


def reference(query, keys_words, keys_scales, lam, pull, old, fade, offs, offs2, offs3):
    idx = unstriped8(offs)
    idx2 = unstriped8(offs2)
    idx3 = unstriped8(offs3)
    keysu = unpack_weight(keys_words, keys_scales, "e2m1")
    queryq = mxq(f64(query), 0, "e4m3")
    a = queryq.T @ keysu
    s = pick8(a, idx, 16) + np.tanh(pick8(a, idx2, 16) - pick8(a, idx3, 16)) * f64(lam)
    p = np.exp(s - np.max(s, axis=1, keepdims=True))
    r = p / np.sum(p, axis=1, keepdims=True)
    r1 = np.pad(r, ((0, 0), (1, 0)))[:, :I]
    w = r - r1 * f64(pull)
    ws = w * 256.0
    wf = np.zeros((Q, T))
    wf[np.arange(Q)[:, None], idx[np.arange(Q) % 128 // 16]] = ws
    y = f64(old) * f64(fade) + wf
    return y

from contextlib import ExitStack

import concourse.mybir as mybir

D, T, I, Q = 512, 1024, 512, 128
FLOPS = 2 * D * T * Q

F32 = mybir.dt.float32
BF16 = mybir.dt.bfloat16
I32 = mybir.dt.int32
U32 = mybir.dt.uint32
U16 = mybir.dt.uint16
U8 = mybir.dt.uint8
FP8X4 = mybir.dt.float8_e4m3fn_x4
FP4X4 = mybir.dt.float4_e2m1fn_x4
ALU = mybir.AluOpType
ACT = mybir.ActivationFunctionType
AX = mybir.AxisListType

P = 128
PACK = 4
HALF = I // 2
LIST_COLS = I // 16
N_PASS = 256
Q_ON_SCALAR = 48
LAG_PAD = 8
STORES = 2


def tile_attend_seconded_stepwise_counts_heads_kernel(
    tc, query, keys_words, keys_scales, lam, pull, old, fade, offs, offs2, offs3, out
):
    nc = tc.nc
    with ExitStack() as ctx:
        sb = ctx.enter_context(tc.tile_pool(name="sb", bufs=1))
        ps = ctx.enter_context(tc.psum_pool(name="ps", bufs=1))

        own_list = sb.tile([P, LIST_COLS], U16, name="own_list")
        second_list = sb.tile([P, LIST_COLS], U16, name="second_list")
        opp_list = sb.tile([P, LIST_COLS], U16, name="opp_list")
        q_raw = sb.tile([P, PACK, Q], F32, name="q_raw")
        k_words = sb.tile([P, 2 * T], U8, name="k_words", align_bytes=64)
        k_scales = sb.tile([P, T], U8, name="k_scales", align_bytes=64)
        lam_t = sb.tile([P, 1], F32, name="lam_t")
        pull_t = sb.tile([P, 1], F32, name="pull_t")
        fade_t = sb.tile([P, 1], F32, name="fade_t")
        old_t = sb.tile([P, T], F32, name="old_t")
        placed = sb.tile([P, T], F32, name="placed")
        lagged = sb.tile([P, LAG_PAD + I], F32, name="lagged")

        nc.vector.memset(k_scales[:].bitcast(I32), 0)
        nc.sync.dma_start(q_raw[:], query.rearrange("(p j) q -> p j q", j=PACK))
        nc.sync.dma_start(k_words[:].bitcast(I32), keys_words[0].bitcast(I32))
        for quad in range(4):
            nc.sync.dma_start(
                k_scales[32 * quad : 32 * quad + 4, :].bitcast(I32),
                keys_scales[0, 4 * quad : 4 * quad + 4, :].bitcast(I32),
            )
        nc.sync.dma_start(opp_list[:], offs3)
        nc.sync.dma_start(own_list[:], offs)
        nc.sync.dma_start(second_list[:], offs2)
        nc.sync.dma_start(lam_t[:], lam)
        nc.sync.dma_start(pull_t[:], pull)
        nc.sync.dma_start(old_t[:], old)
        nc.sync.dma_start(fade_t[:], fade)
        nc.vector.memset(placed[:], 0.0)
        nc.vector.memset(lagged[:, LAG_PAD - 1 : LAG_PAD], 0.0)

        q_bf = sb.tile([P, Q, PACK], BF16, name="q_bf", align_bytes=64)
        q_view = q_raw[:].rearrange("p j q -> p q j")
        nc.scalar.activation(q_bf[:, :Q_ON_SCALAR, :], q_view[:, :Q_ON_SCALAR, :], ACT.Copy)
        nc.vector.tensor_copy(q_bf[:, Q_ON_SCALAR:, :], q_view[:, Q_ON_SCALAR:, :])
        q_codes = sb.tile([P, Q], U32, name="q_codes", align_bytes=64)
        q_scales = sb.tile([P, Q], U8, name="q_scales", align_bytes=64)
        nc.vector.quantize_mx(
            out=q_codes[:].bitcast(FP8X4), scales=q_scales[:], in_=q_bf[:].rearrange("p q j -> p (q j)")
        )

        a = sb.tile([P, T], F32, name="a")
        for n in range(T // N_PASS):
            cols = slice(n * N_PASS, (n + 1) * N_PASS)
            bank = ps.tile([P, N_PASS], F32, name=f"bank{n}")
            nc.tensor.matmul_mx(
                out=bank[:],
                lhsT=q_codes[:].bitcast(FP8X4),
                lhsT_scale=q_scales[:],
                rhs=k_words[:, 2 * n * N_PASS : 2 * (n + 1) * N_PASS].bitcast(FP4X4),
                rhs_scale=k_scales[:, cols],
                start=True,
                stop=True,
            )
            if n % 2 == 0:
                nc.scalar.activation(a[:, cols], bank[:], ACT.Copy)
            else:
                nc.vector.tensor_copy(a[:, cols], bank[:])

        lo, hi = slice(0, HALF), slice(HALF, I)
        lo_l, hi_l = slice(0, LIST_COLS // 2), slice(LIST_COLS // 2, LIST_COLS)

        opp = sb.tile([P, I], F32, name="opp")
        own = sb.tile([P, I], F32, name="own")
        diff = sb.tile([P, I], F32, name="diff")
        vote = sb.tile([P, I], F32, name="vote")
        score = sb.tile([P, I], F32, name="score", tag="score_then_faded")
        nc.scalar.activation(opp[:, lo], a[:].indirect(opp_list[:, lo_l]), ACT.Copy)
        nc.vector.tensor_copy(own[:, lo], a[:].indirect(own_list[:, lo_l]))
        nc.scalar.activation(opp[:, hi], a[:].indirect(opp_list[:, hi_l]), ACT.Copy)
        nc.vector.tensor_tensor(diff[:, lo], a[:].indirect(second_list[:, lo_l]), opp[:, lo], ALU.subtract)
        nc.vector.tensor_tensor(diff[:, hi], a[:].indirect(second_list[:, hi_l]), opp[:, hi], ALU.subtract)
        nc.scalar.activation(vote[:, lo], diff[:, lo], ACT.Tanh)
        nc.scalar.activation(own[:, hi], a[:].indirect(own_list[:, hi_l]), ACT.Copy)
        nc.scalar.activation(vote[:, hi], diff[:, hi], ACT.Tanh)

        neg_max_lo = sb.tile([P, 1], F32, name="neg_max_lo")
        neg_max = sb.tile([P, 1], F32, name="neg_max")
        neg_score_hi = sb.tile([P, HALF], F32, name="neg_score_hi")
        nc.vector.scalar_tensor_tensor(score[:, lo], vote[:, lo], lam_t[:], own[:, lo], ALU.mult, ALU.add)
        nc.vector.tensor_reduce(neg_max_lo[:], score[:, lo], AX.X, ALU.max, negate=True)
        nc.vector.scalar_tensor_tensor(score[:, hi], vote[:, hi], lam_t[:], own[:, hi], ALU.mult, ALU.add)
        nc.vector.tensor_scalar(
            neg_score_hi[:], score[:, hi], -1.0, neg_max_lo[:], ALU.mult, ALU.min, accum_out=neg_max[:]
        )

        neg_pull = sb.tile([P, 1], F32, name="neg_pull")
        nc.gpsimd.tensor_scalar(neg_pull[:], pull_t[:], -1.0, 0.0, ALU.mult, ALU.add)

        p = sb.tile([P, I], F32, name="p")
        sum_lo = sb.tile([P, 1], F32, name="sum_lo")
        sum_hi = sb.tile([P, 1], F32, name="sum_hi")
        total = sb.tile([P, 1], F32, name="total")
        total_256th = sb.tile([P, 1], F32, name="total_256th")
        row_factor = sb.tile([P, 1], F32, name="row_factor")
        nc.scalar.activation(p[:, lo], score[:, lo], ACT.Exp, bias=neg_max[:], accum_out=sum_lo[:])
        nc.vector.tensor_scalar(lagged[:, LAG_PAD : LAG_PAD + HALF], p[:, lo], neg_pull[:], None, ALU.mult)
        nc.vector.tensor_tensor(
            placed[:].indirect(own_list[:, lo_l]), p[:, lo], lagged[:, LAG_PAD - 1 : LAG_PAD - 1 + HALF], ALU.add
        )
        nc.scalar.activation(p[:, hi], neg_score_hi[:], ACT.Exp, bias=neg_max[:], scale=-1.0, accum_out=sum_hi[:])
        nc.scalar.activation(total[:], sum_lo[:], ACT.Identity, bias=sum_hi[:])
        nc.scalar.activation(total_256th[:], total[:], ACT.Copy, scale=1.0 / 256.0)
        nc.scalar.activation(
            lagged[:, LAG_PAD + HALF : LAG_PAD + I - 1], p[:, HALF : I - 1], ACT.Copy, scale=neg_pull[:]
        )
        nc.vector.reciprocal(row_factor[:], total_256th[:])
        nc.vector.tensor_tensor(
            placed[:].indirect(own_list[:, hi_l]),
            p[:, hi],
            lagged[:, LAG_PAD - 1 + HALF : LAG_PAD - 1 + I],
            ALU.add,
        )

        faded = sb.tile([P, T], F32, name="faded", tag="score_then_faded")
        nc.scalar.activation(faded[:], old_t[:], ACT.Copy, scale=fade_t[:])
        result = sb.tile([P, T], F32, name="result")
        width = T // STORES
        for n in range(STORES):
            cols = slice(n * width, (n + 1) * width)
            nc.vector.scalar_tensor_tensor(
                result[:, cols], placed[:, cols], row_factor[:], faded[:, cols], ALU.mult, ALU.add
            )
            queue = nc.sync if n % 2 == 0 else nc.scalar
            queue.dma_start(out[:, cols], result[:, cols])
